import numpy as np
import ml_dtypes


def mxq(x, axis, fmt="e4m3"):
    dtype, down = {"e4m3": (ml_dtypes.float8_e4m3fn, 7), "e5m2": (ml_dtypes.float8_e5m2, 14)}[fmt]
    v = np.moveaxis(np.asarray(x, np.float32).astype(ml_dtypes.bfloat16).astype(np.float64), axis, -1)
    blocks = v.reshape(v.shape[:-1] + (-1, 32))
    amax = np.abs(blocks).max(-1, keepdims=True)
    byte = np.maximum(np.where(amax > 0, np.frexp(amax)[1] - 1 + 127, 0) - down, 1)
    scale = np.exp2(byte - 127.0)
    codes = (blocks / scale).astype(np.float32).astype(dtype).astype(np.float64)
    return np.moveaxis((codes * scale).reshape(v.shape), -1, axis)


WIDE = False


def mx_kscale(k):
    if not WIDE:
        return np.ones(k)
    levels = np.array([10, -10, 5, -5, 0])
    if k % 512:
        return np.exp2(np.random.permutation(np.resize(levels, k // 32))).repeat(32)
    a = np.empty((k // 512, 16))
    for p in range(k // 512):
        a[p, :8] = np.random.permutation(np.resize(levels, 8))
        for g in range(8):
            far = levels[np.abs(levels - a[p, g]) >= 10]
            a[p, g + 8] = far[np.random.randint(len(far))]
    return np.exp2(a.ravel()).repeat(32)


def f64(x):
    return np.asarray(x).astype(np.float64)


def striped8(idx):
    return np.asarray(idx).reshape(8, -1, 16).transpose(0, 2, 1).reshape(128, -1).astype(np.uint16)


def unstriped8(offs):
    return offs.reshape(8, 16, -1).transpose(0, 2, 1).reshape(8, -1).astype(np.int64)


def pick8(x, idx, run):
    r = np.arange(len(x))
    return x[r[:, None], idx[r % (8 * run) // run]]


E2M1 = np.array([0.0, 0.5, 1.0, 1.5, 2.0, 3.0, 4.0, 6.0, -0.0, -0.5, -1.0, -1.5, -2.0, -3.0, -4.0, -6.0])


def pack_weight(w, fmt):
    k, n = w.shape
    w = f64(np.asarray(w, np.float32).astype(ml_dtypes.bfloat16)).reshape(k // 32, 32, n)
    amax = np.abs(w).max(1)
    if fmt == "e4m3":
        byte = np.frexp(amax)[1] - 1 + 127 - 7
    else:
        mant, ex = np.frexp(amax / 6.0)
        byte = np.where(mant > 0.5, ex, ex - 1) + 127
    byte = np.clip(np.where(amax > 0, byte, 1), 1, 254)
    scaled = (w * np.exp2(127.0 - byte)[:, None, :]).reshape(k, n).astype(np.float32)
    by_word = np.ascontiguousarray(scaled.reshape(k // 512, 128, 4, n).transpose(0, 1, 3, 2))
    if fmt == "e4m3":
        words = by_word.astype(ml_dtypes.float8_e4m3fn).view(np.uint8)
    else:
        c = by_word.astype(ml_dtypes.float4_e2m1fn).view(np.uint8) & 0xF
        words = (c[..., 0::2] | (c[..., 1::2] << 4)).reshape(k // 512, 128, 2 * n)
    return np.ascontiguousarray(words), np.ascontiguousarray(byte.astype(np.uint8).reshape(k // 512, 16, n))


def unpack_weight(words, scales, fmt):
    g, _, n = scales.shape
    words = np.ascontiguousarray(words).reshape(g, 128, n, -1)
    if fmt == "e4m3":
        vals = words.view(ml_dtypes.float8_e4m3fn).astype(np.float64)
    else:
        nib = np.empty((g, 128, n, 4), np.uint8)
        nib[..., 0::2] = words & 0xF
        nib[..., 1::2] = words >> 4
        vals = E2M1[nib]
    vals = vals * np.repeat(np.exp2(scales.astype(np.float64) - 127.0), 8, axis=1)[..., None]
    return vals.transpose(0, 1, 3, 2).reshape(g * 512, n)


def softplus(v):
    return np.log(1.0 + np.exp(v))


D, T, I, Q = 512, 1024, 512, 128


def setup_inputs():
    n = np.random.standard_normal
    idx = np.stack([np.random.permutation(T)[:I] for _ in range(8)])
    idx2 = np.stack([np.random.permutation(T)[:I] for _ in range(8)])
    idx3 = np.stack([np.random.permutation(T)[:I] for _ in range(8)])
    idx4 = np.stack([np.random.permutation(T)[:I] for _ in range(8)])
    fd = mx_kscale(D)
    keysp = pack_weight(n((D, T)) / fd[:, None], "e4m3")
    return {
        "query": (n((D, Q)) * 0.9 / np.sqrt(D) * fd[:, None]).astype(np.float32),
        "query2": (n((D, Q)) * 0.9 / np.sqrt(D) * fd[:, None]).astype(np.float32),
        "keys_words": keysp[0],
        "keys_scales": keysp[1],
        "lam": (np.random.uniform(0.6, 1.2, (Q, 1))).astype(np.float32),
        "old": (1.0 * n((Q, T))).astype(np.float32),
        "offs": striped8(idx),
        "offs2": striped8(idx2),
        "offs3": striped8(idx3),
        "offs4": striped8(idx4),
    }


def reference(query, query2, keys_words, keys_scales, lam, old, offs, offs2, offs3, offs4):
    idx = unstriped8(offs)
    idx2 = unstriped8(offs2)
    idx3 = unstriped8(offs3)
    idx4 = unstriped8(offs4)
    keysu = unpack_weight(keys_words, keys_scales, "e4m3")
    queryq = mxq(f64(query), 0, "e4m3")
    a = queryq.T @ keysu
    query2q = mxq(f64(query2), 0, "e4m3")
    b = query2q.T @ keysu
    w = pick8(a, idx, 16) / (softplus(pick8(b, idx2, 16)) + 0.5) * f64(lam)
    f1 = np.zeros((Q, T))
    f1[np.arange(Q)[:, None], idx[np.arange(Q) % 128 // 16]] = w
    f2 = f1 + f64(old)
    y = np.maximum(pick8(f2, idx3, 16), pick8(f2, idx4, 16))
    return y

@@ -1,0 +1,160 @@
+import math
+from contextlib import ExitStack
+
+import concourse.mybir as mybir
+
+D, T, I, Q = 512, 1024, 512, 128
+FLOPS = 2 * 2 * D * T * Q
+
+F32 = mybir.dt.float32
+BF16 = mybir.dt.bfloat16
+I32 = mybir.dt.int32
+U32 = mybir.dt.uint32
+U16 = mybir.dt.uint16
+U8 = mybir.dt.uint8
+FP8X4 = mybir.dt.float8_e4m3fn_x4
+ALU = mybir.AluOpType
+ACT = mybir.ActivationFunctionType
+
+P = 128
+PACK = 4
+CHUNKS = 4
+N = T // CHUNKS
+BANK = 512
+HALF = I // 2
+QUARTER = I // 4
+EXP_CAP = 2.0 ** 60
+
+
+def tile_attend_worthfor_lean_throughtwo_heads_kernel(
+    tc, query, query2, keys_words, keys_scales, lam, old, offs, offs2, offs3, offs4, out
+):
+    nc = tc.nc
+    with ExitStack() as ctx:
+        sb = ctx.enter_context(tc.tile_pool(name="sb", bufs=1))
+        ps = ctx.enter_context(tc.psum_pool(name="ps", bufs=1))
+
+        def listed(window, lst, lo, hi):
+            return window[:].indirect(lst[:, lo // 16 : hi // 16])
+
+        key_scales = sb.tile([P, N], U8, name="key_scales", align_bytes=64)
+        nc.gpsimd.memset(key_scales[:].bitcast(I32), 0)
+
+        raw2 = sb.tile([P, PACK, Q], F32, name="raw2")
+        nc.sync.dma_start(out=raw2[:], in_=query2.rearrange("(p j) q -> p j q", j=PACK))
+        for quad in range(4):
+            rows = keys_scales[0, 4 * quad : 4 * quad + 4, :].bitcast(I32)
+            nc.scalar.dma_start(
+                out=key_scales[32 * quad : 32 * quad + 16, :].bitcast(I32),
+                in_=rows.rearrange("r (c n) -> c r n", c=CHUNKS),
+            )
+        words_hbm = keys_words[0].rearrange("p n t -> p (n t)").bitcast(I32)
+        key_words = []
+        for h in range(2):
+            words = sb.tile([P, BANK], U32, name="key_words%d" % h, align_bytes=64)
+            nc.sync.dma_start(out=words[:].bitcast(I32), in_=words_hbm[:, h * BANK : (h + 1) * BANK])
+            key_words.append(words)
+        list2 = sb.tile([P, I // 16], U16, name="list2")
+        nc.sync.dma_start(list2[:], offs2)
+        raw1 = sb.tile([P, PACK, Q], F32, name="raw1")
+        nc.sync.dma_start(out=raw1[:], in_=query.rearrange("(p j) q -> p j q", j=PACK))
+        list1 = sb.tile([P, I // 16], U16, name="list1")
+        nc.sync.dma_start(list1[:], offs)
+        lam_col = sb.tile([P, 1], F32, name="lam_col")
+        nc.sync.dma_start(out=lam_col[:], in_=lam)
+        old_sb = sb.tile([P, T], F32, name="old_sb")
+        nc.sync.dma_start(out=old_sb[:], in_=old)
+        list3 = sb.tile([P, I // 16], U16, name="list3")
+        nc.sync.dma_start(list3[:], offs3)
+        list4 = sb.tile([P, I // 16], U16, name="list4")
+        nc.sync.dma_start(list4[:], offs4)
+
+        f1 = sb.tile([P, T], F32, name="f1")
+        nc.gpsimd.memset(f1[:], 0.0)
+
+        def quantise(grouped, tag):
+            codes = sb.tile([P, Q], U32, name="codes" + tag, align_bytes=64)
+            scales = sb.tile([P, Q], U8, name="scales" + tag, align_bytes=64)
+            nc.vector.quantize_mx(
+                out=codes[:].bitcast(FP8X4),
+                scales=scales[:],
+                in_=grouped[:].rearrange("p q j -> p (q j)"),
+            )
+            return codes, scales
+
+        def score(acc, codes, scales, c):
+            nc.tensor.matmul_mx(
+                out=acc,
+                lhsT=codes[:].bitcast(FP8X4),
+                lhsT_scale=scales[:],
+                rhs=key_words[c // 2][:, (c % 2) * N : (c % 2 + 1) * N].bitcast(FP8X4),
+                rhs_scale=key_scales[4 * c : P, :],
+                start=True,
+                stop=True,
+            )
+
+        grouped2 = sb.tile([P, Q, PACK], BF16, name="grouped2", align_bytes=64)
+        nc.vector.tensor_copy(out=grouped2[:], in_=raw2[:].rearrange("p j q -> p q j"))
+        codes2, scales2 = quantise(grouped2, "2")
+        b_sb = sb.tile([P, T], F32, name="b_sb", tag="scores")
+        for c in range(CHUNKS):
+            bank = ps.tile([P, BANK], F32, name="b_bank%d" % c)
+            score(bank[:, 0:N], codes2, scales2, c)
+            if c % 2 == 0:
+                nc.scalar.activation(b_sb[:, c * N : (c + 1) * N], bank[:, 0:N], ACT.Copy)
+            else:
+                nc.vector.tensor_copy(b_sb[:, c * N : (c + 1) * N], bank[:, 0:N])
+
+        x = sb.tile([P, I], F32, name="x")
+        e = sb.tile([P, I], F32, name="e")
+        nc.scalar.activation(e[:, 0:HALF], listed(b_sb, list2, 0, HALF), ACT.Exp)
+        nc.vector.tensor_copy(x[:, HALF:I], listed(b_sb, list2, HALF, I))
+        nc.scalar.activation(e[:, HALF:I], x[:, HALF:I], ACT.Exp)
+
+        grouped1 = sb.tile([P, Q, PACK], BF16, name="grouped1", align_bytes=64)
+        nc.gpsimd.tensor_copy(out=grouped1[:], in_=raw1[:].rearrange("p j q -> p q j"))
+        codes1, scales1 = quantise(grouped1, "1")
+        nc.vector.tensor_copy(x[:, 0:HALF], listed(b_sb, list2, 0, HALF))
+        e1 = sb.tile([P, I], F32, name="e1")
+        nc.vector.tensor_scalar(e1[:], e[:], EXP_CAP, 1.0, ALU.min, ALU.add)
+        a_sb = sb.tile([P, T], F32, name="a_sb", tag="scores")
+        for h in range(2):
+            bank = ps.tile([P, BANK], F32, name="a_bank%d" % h)
+            for c in (2 * h, 2 * h + 1):
+                score(bank[:, (c % 2) * N : (c % 2 + 1) * N], codes1, scales1, c)
+            nc.vector.tensor_copy(a_sb[:, h * BANK : (h + 1) * BANK], bank[:])
+
+        capped = sb.tile([P, I], F32, name="capped")
+        den = sb.tile([P, I], F32, name="den")
+        for lo in (0, HALF):
+            s = slice(lo, lo + HALF)
+            nc.scalar.activation(capped[:, s], e1[:, s], ACT.Ln, scale=math.exp(0.5))
+            nc.vector.scalar_tensor_tensor(den[:, s], x[:, s], 0.5, capped[:, s], ALU.add, ALU.max)
+
+        ag = sb.tile([P, I], F32, name="ag")
+        nc.vector.tensor_copy(ag[:], a_sb[:].indirect(list1[:]))
+        num = sb.tile([P, I], F32, name="num")
+        nc.vector.tensor_scalar(num[:], ag[:], lam_col[:], None, ALU.mult)
+
+        root = sb.tile([P, I], F32, name="root")
+        inv = sb.tile([P, I], F32, name="inv")
+        for lo, hi in ((0, QUARTER), (QUARTER, HALF), (HALF, I)):
+            s = slice(lo, hi)
+            nc.scalar.activation(root[:, s], den[:, s], ACT.Abs_reciprocal_sqrt)
+            nc.scalar.activation(inv[:, s], root[:, s], ACT.Square)
+        for lo, hi in ((0, QUARTER), (QUARTER, I)):
+            s = slice(lo, hi)
+            nc.vector.tensor_tensor(listed(f1, list1, lo, hi), num[:, s], inv[:, s], ALU.mult)
+
+        f2 = sb.tile([P, T], F32, name="f2")
+        nc.vector.tensor_tensor(f2[:], f1[:], old_sb[:], ALU.add)
+
+        g3 = sb.tile([P, I], F32, name="g3")
+        g4 = sb.tile([P, I], F32, name="g4")
+        y = sb.tile([P, I], F32, name="y")
+        for lo in (0, HALF):
+            s = slice(lo, lo + HALF)
+            nc.scalar.activation(g4[:, s], listed(f2, list4, lo, lo + HALF), ACT.Copy)
+            nc.vector.tensor_copy(g3[:, s], listed(f2, list3, lo, lo + HALF))
+            nc.vector.tensor_tensor(y[:, s], g3[:, s], g4[:, s], ALU.max)
+            nc.sync.dma_start(out=out[:, s], in_=y[:, s])

@@ -23,6 +23,7 @@ N = T // CHUNKS
 BANK = 512
 HALF = I // 2
 QUARTER = I // 4
+OWN = 352
 EXP_CAP = 2.0 ** 60
 
 
@@ -37,16 +38,16 @@ def tile_attend_worthfor_lean_throughtwo_heads_kernel(
         def listed(window, lst, lo, hi):
             return window[:].indirect(lst[:, lo // 16 : hi // 16])
 
-        key_scales = sb.tile([P, N], U8, name="key_scales", align_bytes=64)
-        nc.gpsimd.memset(key_scales[:].bitcast(I32), 0)
+        key_scales = sb.tile([P, T], U8, name="key_scales", align_bytes=64)
 
         raw2 = sb.tile([P, PACK, Q], F32, name="raw2")
         nc.sync.dma_start(out=raw2[:], in_=query2.rearrange("(p j) q -> p j q", j=PACK))
         for quad in range(4):
             rows = keys_scales[0, 4 * quad : 4 * quad + 4, :].bitcast(I32)
-            nc.scalar.dma_start(
-                out=key_scales[32 * quad : 32 * quad + 16, :].bitcast(I32),
-                in_=rows.rearrange("r (c n) -> c r n", c=CHUNKS),
+            queue = nc.scalar if quad < 2 else nc.sync
+            queue.dma_start(
+                out=key_scales[32 * quad : 32 * quad + 4, :].bitcast(I32),
+                in_=rows,
             )
         words_hbm = keys_words[0].rearrange("p n t -> p (n t)").bitcast(I32)
         key_words = []
@@ -54,10 +55,10 @@ def tile_attend_worthfor_lean_throughtwo_heads_kernel(
             words = sb.tile([P, BANK], U32, name="key_words%d" % h, align_bytes=64)
             nc.sync.dma_start(out=words[:].bitcast(I32), in_=words_hbm[:, h * BANK : (h + 1) * BANK])
             key_words.append(words)
-        list2 = sb.tile([P, I // 16], U16, name="list2")
-        nc.sync.dma_start(list2[:], offs2)
         raw1 = sb.tile([P, PACK, Q], F32, name="raw1")
         nc.sync.dma_start(out=raw1[:], in_=query.rearrange("(p j) q -> p j q", j=PACK))
+        list2 = sb.tile([P, I // 16], U16, name="list2")
+        nc.sync.dma_start(list2[:], offs2)
         list1 = sb.tile([P, I // 16], U16, name="list1")
         nc.sync.dma_start(list1[:], offs)
         lam_col = sb.tile([P, 1], F32, name="lam_col")
@@ -88,7 +89,7 @@ def tile_attend_worthfor_lean_throughtwo_heads_kernel(
                 lhsT=codes[:].bitcast(FP8X4),
                 lhsT_scale=scales[:],
                 rhs=key_words[c // 2][:, (c % 2) * N : (c % 2 + 1) * N].bitcast(FP8X4),
-                rhs_scale=key_scales[4 * c : P, :],
+                rhs_scale=key_scales[:, c * N : (c + 1) * N],
                 start=True,
                 stop=True,
             )
@@ -96,49 +97,52 @@ def tile_attend_worthfor_lean_throughtwo_heads_kernel(
         grouped2 = sb.tile([P, Q, PACK], BF16, name="grouped2", align_bytes=64)
         nc.vector.tensor_copy(out=grouped2[:], in_=raw2[:].rearrange("p j q -> p q j"))
         codes2, scales2 = quantise(grouped2, "2")
-        b_sb = sb.tile([P, T], F32, name="b_sb", tag="scores")
+        grouped1 = sb.tile([P, Q, PACK], BF16, name="grouped1", align_bytes=64)
+        nc.gpsimd.tensor_copy(out=grouped1[:], in_=raw1[:].rearrange("p j q -> p q j"))
+        b_sb = sb.tile([P, T], F32, name="b_sb")
         for c in range(CHUNKS):
-            bank = ps.tile([P, BANK], F32, name="b_bank%d" % c)
+            if c < CHUNKS - 1:
+                bank = ps.tile([P, BANK], F32, name="b_bank%d" % c)
+            else:
+                bank = ps.tile([P, T], F32, name="b_last", tag="late")
             score(bank[:, 0:N], codes2, scales2, c)
             if c % 2 == 0:
                 nc.scalar.activation(b_sb[:, c * N : (c + 1) * N], bank[:, 0:N], ACT.Copy)
             else:
                 nc.vector.tensor_copy(b_sb[:, c * N : (c + 1) * N], bank[:, 0:N])
-
-        x = sb.tile([P, I], F32, name="x")
-        e = sb.tile([P, I], F32, name="e")
-        nc.scalar.activation(e[:, 0:HALF], listed(b_sb, list2, 0, HALF), ACT.Exp)
-        nc.vector.tensor_copy(x[:, HALF:I], listed(b_sb, list2, HALF, I))
-        nc.scalar.activation(e[:, HALF:I], x[:, HALF:I], ACT.Exp)
-
-        grouped1 = sb.tile([P, Q, PACK], BF16, name="grouped1", align_bytes=64)
-        nc.gpsimd.tensor_copy(out=grouped1[:], in_=raw1[:].rearrange("p j q -> p q j"))
         codes1, scales1 = quantise(grouped1, "1")
-        nc.vector.tensor_copy(x[:, 0:HALF], listed(b_sb, list2, 0, HALF))
+
+        x_lo = sb.tile([P, HALF], F32, name="x_lo")
+        x_hi = sb.tile([P, HALF], F32, name="x_hi")
+        e = sb.tile([P, I], F32, name="e")
+        nc.scalar.activation(e[:, 0:OWN], listed(b_sb, list2, 0, OWN), ACT.Exp)
+        nc.vector.tensor_copy(x_hi[:], listed(b_sb, list2, HALF, I))
+        nc.scalar.activation(e[:, OWN:I], x_hi[:, OWN - HALF : HALF], ACT.Exp)
+        nc.vector.tensor_copy(x_lo[:], listed(b_sb, list2, 0, HALF))
+
+        a_sb = sb.tile([P, T], F32, name="a_sb")
+        a_banks = ps.tile([P, T], F32, name="a_banks", tag="late")
+        for c in range(CHUNKS):
+            score(a_banks[:, c * N : (c + 1) * N], codes1, scales1, c)
+        for h in range(2):
+            nc.vector.tensor_copy(a_sb[:, h * BANK : (h + 1) * BANK], a_banks[:, h * BANK : (h + 1) * BANK])
         e1 = sb.tile([P, I], F32, name="e1")
         nc.vector.tensor_scalar(e1[:], e[:], EXP_CAP, 1.0, ALU.min, ALU.add)
-        a_sb = sb.tile([P, T], F32, name="a_sb", tag="scores")
-        for h in range(2):
-            bank = ps.tile([P, BANK], F32, name="a_bank%d" % h)
-            for c in (2 * h, 2 * h + 1):
-                score(bank[:, (c % 2) * N : (c % 2 + 1) * N], codes1, scales1, c)
-            nc.vector.tensor_copy(a_sb[:, h * BANK : (h + 1) * BANK], bank[:])
+        ag = sb.tile([P, I], F32, name="ag")
+        nc.vector.tensor_copy(ag[:], a_sb[:].indirect(list1[:]))
 
         capped = sb.tile([P, I], F32, name="capped")
         den = sb.tile([P, I], F32, name="den")
-        for lo in (0, HALF):
+        num = sb.tile([P, I], F32, name="num")
+        for lo, x in ((0, x_lo), (HALF, x_hi)):
             s = slice(lo, lo + HALF)
             nc.scalar.activation(capped[:, s], e1[:, s], ACT.Ln, scale=math.exp(0.5))
-            nc.vector.scalar_tensor_tensor(den[:, s], x[:, s], 0.5, capped[:, s], ALU.add, ALU.max)
-
-        ag = sb.tile([P, I], F32, name="ag")
-        nc.vector.tensor_copy(ag[:], a_sb[:].indirect(list1[:]))
-        num = sb.tile([P, I], F32, name="num")
+            nc.vector.scalar_tensor_tensor(den[:, s], x[:], 0.5, capped[:, s], ALU.add, ALU.max)
         nc.vector.tensor_scalar(num[:], ag[:], lam_col[:], None, ALU.mult)
 
         root = sb.tile([P, I], F32, name="root")
         inv = sb.tile([P, I], F32, name="inv")
-        for lo, hi in ((0, QUARTER), (QUARTER, HALF), (HALF, I)):
+        for lo, hi in ((0, QUARTER), (QUARTER, I - QUARTER), (I - QUARTER, I)):
             s = slice(lo, hi)
             nc.scalar.activation(root[:, s], den[:, s], ACT.Abs_reciprocal_sqrt)
             nc.scalar.activation(inv[:, s], root[:, s], ACT.Square)

@@ -18,12 +18,13 @@ ACT = mybir.ActivationFunctionType
 
 P = 128
 PACK = 4
+QUADRANTS = 4
+GROUP = 16
+BANK = 512
 CHUNKS = 4
 N = T // CHUNKS
-BANK = 512
 HALF = I // 2
 QUARTER = I // 4
-OWN = 352
 EXP_CAP = 2.0 ** 60
 
 
@@ -35,16 +36,16 @@ def tile_attend_worthfor_lean_throughtwo_heads_kernel(
         sb = ctx.enter_context(tc.tile_pool(name="sb", bufs=1))
         ps = ctx.enter_context(tc.psum_pool(name="ps", bufs=1))
 
-        def listed(window, lst, lo, hi):
-            return window[:].indirect(lst[:, lo // 16 : hi // 16])
+        def listed(window, entries, lo, hi):
+            return window[:].indirect(entries[:, lo // GROUP : hi // GROUP])
 
         key_scales = sb.tile([P, T], U8, name="key_scales", align_bytes=64)
 
         raw2 = sb.tile([P, PACK, Q], F32, name="raw2")
         nc.sync.dma_start(out=raw2[:], in_=query2.rearrange("(p j) q -> p j q", j=PACK))
-        for quad in range(4):
+        for quad in range(QUADRANTS):
             rows = keys_scales[0, 4 * quad : 4 * quad + 4, :].bitcast(I32)
-            queue = nc.scalar if quad < 2 else nc.sync
+            queue = nc.scalar if quad < QUADRANTS // 2 else nc.sync
             queue.dma_start(
                 out=key_scales[32 * quad : 32 * quad + 4, :].bitcast(I32),
                 in_=rows,
@@ -52,30 +53,32 @@ def tile_attend_worthfor_lean_throughtwo_heads_kernel(
         words_hbm = keys_words[0].rearrange("p n t -> p (n t)").bitcast(I32)
         key_words = []
         for h in range(2):
-            words = sb.tile([P, BANK], U32, name="key_words%d" % h, align_bytes=64)
-            nc.sync.dma_start(out=words[:].bitcast(I32), in_=words_hbm[:, h * BANK : (h + 1) * BANK])
+            words = sb.tile([P, T // 2], U32, name="key_words%d" % h, align_bytes=64)
+            nc.sync.dma_start(
+                out=words[:].bitcast(I32), in_=words_hbm[:, h * (T // 2) : (h + 1) * (T // 2)]
+            )
             key_words.append(words)
         raw1 = sb.tile([P, PACK, Q], F32, name="raw1")
         nc.sync.dma_start(out=raw1[:], in_=query.rearrange("(p j) q -> p j q", j=PACK))
-        list2 = sb.tile([P, I // 16], U16, name="list2")
+        list2 = sb.tile([P, I // GROUP], U16, name="list2")
         nc.sync.dma_start(list2[:], offs2)
-        list1 = sb.tile([P, I // 16], U16, name="list1")
+        list1 = sb.tile([P, I // GROUP], U16, name="list1")
         nc.sync.dma_start(list1[:], offs)
         lam_col = sb.tile([P, 1], F32, name="lam_col")
         nc.sync.dma_start(out=lam_col[:], in_=lam)
         old_sb = sb.tile([P, T], F32, name="old_sb")
         nc.sync.dma_start(out=old_sb[:], in_=old)
-        list3 = sb.tile([P, I // 16], U16, name="list3")
+        list3 = sb.tile([P, I // GROUP], U16, name="list3")
         nc.sync.dma_start(list3[:], offs3)
-        list4 = sb.tile([P, I // 16], U16, name="list4")
+        list4 = sb.tile([P, I // GROUP], U16, name="list4")
         nc.sync.dma_start(list4[:], offs4)
 
         f1 = sb.tile([P, T], F32, name="f1")
         nc.gpsimd.memset(f1[:], 0.0)
 
-        def quantise(grouped, tag):
-            codes = sb.tile([P, Q], U32, name="codes" + tag, align_bytes=64)
-            scales = sb.tile([P, Q], U8, name="scales" + tag, align_bytes=64)
+        def quantise(grouped, suffix):
+            codes = sb.tile([P, Q], U32, name="codes" + suffix, align_bytes=64)
+            scales = sb.tile([P, Q], U8, name="scales" + suffix, align_bytes=64)
             nc.vector.quantize_mx(
                 out=codes[:].bitcast(FP8X4),
                 scales=scales[:],
@@ -106,38 +109,35 @@ def tile_attend_worthfor_lean_throughtwo_heads_kernel(
             else:
                 bank = ps.tile([P, T], F32, name="b_last", tag="late")
             score(bank[:, 0:N], codes2, scales2, c)
-            if c % 2 == 0:
+            if c in (0, CHUNKS - 1):
                 nc.scalar.activation(b_sb[:, c * N : (c + 1) * N], bank[:, 0:N], ACT.Copy)
             else:
                 nc.vector.tensor_copy(b_sb[:, c * N : (c + 1) * N], bank[:, 0:N])
         codes1, scales1 = quantise(grouped1, "1")
 
-        x_lo = sb.tile([P, HALF], F32, name="x_lo")
-        x_hi = sb.tile([P, HALF], F32, name="x_hi")
+        x = sb.tile([P, I], F32, name="x")
         e = sb.tile([P, I], F32, name="e")
-        nc.scalar.activation(e[:, 0:OWN], listed(b_sb, list2, 0, OWN), ACT.Exp)
-        nc.vector.tensor_copy(x_hi[:], listed(b_sb, list2, HALF, I))
-        nc.scalar.activation(e[:, OWN:I], x_hi[:, OWN - HALF : HALF], ACT.Exp)
-        nc.vector.tensor_copy(x_lo[:], listed(b_sb, list2, 0, HALF))
+        nc.scalar.activation(e[:], b_sb[:].indirect(list2[:]), ACT.Exp)
+        nc.vector.tensor_copy(x[:], b_sb[:].indirect(list2[:]))
 
         a_sb = sb.tile([P, T], F32, name="a_sb")
         a_banks = ps.tile([P, T], F32, name="a_banks", tag="late")
         for c in range(CHUNKS):
             score(a_banks[:, c * N : (c + 1) * N], codes1, scales1, c)
-        for h in range(2):
-            nc.vector.tensor_copy(a_sb[:, h * BANK : (h + 1) * BANK], a_banks[:, h * BANK : (h + 1) * BANK])
+        nc.vector.tensor_copy(a_sb[:, 0:BANK], a_banks[:, 0:BANK])
         e1 = sb.tile([P, I], F32, name="e1")
         nc.vector.tensor_scalar(e1[:], e[:], EXP_CAP, 1.0, ALU.min, ALU.add)
+        nc.vector.tensor_copy(a_sb[:, BANK:T], a_banks[:, BANK:T])
         ag = sb.tile([P, I], F32, name="ag")
         nc.vector.tensor_copy(ag[:], a_sb[:].indirect(list1[:]))
 
         capped = sb.tile([P, I], F32, name="capped")
         den = sb.tile([P, I], F32, name="den")
         num = sb.tile([P, I], F32, name="num")
-        for lo, x in ((0, x_lo), (HALF, x_hi)):
+        for lo in (0, HALF):
             s = slice(lo, lo + HALF)
             nc.scalar.activation(capped[:, s], e1[:, s], ACT.Ln, scale=math.exp(0.5))
-            nc.vector.scalar_tensor_tensor(den[:, s], x[:], 0.5, capped[:, s], ALU.add, ALU.max)
+            nc.vector.scalar_tensor_tensor(den[:, s], x[:, s], 0.5, capped[:, s], ALU.add, ALU.max)
         nc.vector.tensor_scalar(num[:], ag[:], lam_col[:], None, ALU.mult)
 
         root = sb.tile([P, I], F32, name="root")

import math
from contextlib import ExitStack

import concourse.mybir as mybir

D, T, I, Q = 512, 1024, 512, 128
FLOPS = 2 * 2 * D * T * Q

F32 = mybir.dt.float32
BF16 = mybir.dt.bfloat16
I32 = mybir.dt.int32
U32 = mybir.dt.uint32
U16 = mybir.dt.uint16
U8 = mybir.dt.uint8
FP8X4 = mybir.dt.float8_e4m3fn_x4
ALU = mybir.AluOpType
ACT = mybir.ActivationFunctionType

P = 128
PACK = 4
QUADRANTS = 4
GROUP = 16
BANK = 512
CHUNKS = 4
N = T // CHUNKS
HALF = I // 2
QUARTER = I // 4
EXP_CAP = 2.0 ** 60


def tile_attend_worthfor_lean_throughtwo_heads_kernel(
    tc, query, query2, keys_words, keys_scales, lam, old, offs, offs2, offs3, offs4, out
):
    nc = tc.nc
    with ExitStack() as ctx:
        sb = ctx.enter_context(tc.tile_pool(name="sb", bufs=1))
        ps = ctx.enter_context(tc.psum_pool(name="ps", bufs=1))

        def listed(window, entries, lo, hi):
            return window[:].indirect(entries[:, lo // GROUP : hi // GROUP])

        key_scales = sb.tile([P, T], U8, name="key_scales", align_bytes=64)

        raw2 = sb.tile([P, PACK, Q], F32, name="raw2")
        nc.sync.dma_start(out=raw2[:], in_=query2.rearrange("(p j) q -> p j q", j=PACK))
        for quad in range(QUADRANTS):
            rows = keys_scales[0, 4 * quad : 4 * quad + 4, :].bitcast(I32)
            queue = nc.scalar if quad < QUADRANTS // 2 else nc.sync
            queue.dma_start(
                out=key_scales[32 * quad : 32 * quad + 4, :].bitcast(I32),
                in_=rows,
            )
        words_hbm = keys_words[0].rearrange("p n t -> p (n t)").bitcast(I32)
        key_words = []
        for h in range(2):
            words = sb.tile([P, T // 2], U32, name="key_words%d" % h, align_bytes=64)
            nc.sync.dma_start(
                out=words[:].bitcast(I32), in_=words_hbm[:, h * (T // 2) : (h + 1) * (T // 2)]
            )
            key_words.append(words)
        raw1 = sb.tile([P, PACK, Q], F32, name="raw1")
        nc.sync.dma_start(out=raw1[:], in_=query.rearrange("(p j) q -> p j q", j=PACK))
        list2 = sb.tile([P, I // GROUP], U16, name="list2")
        nc.sync.dma_start(list2[:], offs2)
        list1 = sb.tile([P, I // GROUP], U16, name="list1")
        nc.sync.dma_start(list1[:], offs)
        lam_col = sb.tile([P, 1], F32, name="lam_col")
        nc.sync.dma_start(out=lam_col[:], in_=lam)
        old_sb = sb.tile([P, T], F32, name="old_sb")
        nc.sync.dma_start(out=old_sb[:], in_=old)
        list3 = sb.tile([P, I // GROUP], U16, name="list3")
        nc.sync.dma_start(list3[:], offs3)
        list4 = sb.tile([P, I // GROUP], U16, name="list4")
        nc.sync.dma_start(list4[:], offs4)

        f1 = sb.tile([P, T], F32, name="f1")
        nc.gpsimd.memset(f1[:], 0.0)

        def quantise(grouped, suffix):
            codes = sb.tile([P, Q], U32, name="codes" + suffix, align_bytes=64)
            scales = sb.tile([P, Q], U8, name="scales" + suffix, align_bytes=64)
            nc.vector.quantize_mx(
                out=codes[:].bitcast(FP8X4),
                scales=scales[:],
                in_=grouped[:].rearrange("p q j -> p (q j)"),
            )
            return codes, scales

        def score(acc, codes, scales, c):
            nc.tensor.matmul_mx(
                out=acc,
                lhsT=codes[:].bitcast(FP8X4),
                lhsT_scale=scales[:],
                rhs=key_words[c // 2][:, (c % 2) * N : (c % 2 + 1) * N].bitcast(FP8X4),
                rhs_scale=key_scales[:, c * N : (c + 1) * N],
                start=True,
                stop=True,
            )

        grouped2 = sb.tile([P, Q, PACK], BF16, name="grouped2", align_bytes=64)
        nc.vector.tensor_copy(out=grouped2[:], in_=raw2[:].rearrange("p j q -> p q j"))
        codes2, scales2 = quantise(grouped2, "2")
        grouped1 = sb.tile([P, Q, PACK], BF16, name="grouped1", align_bytes=64)
        nc.gpsimd.tensor_copy(out=grouped1[:], in_=raw1[:].rearrange("p j q -> p q j"))
        b_sb = sb.tile([P, T], F32, name="b_sb")
        for c in range(CHUNKS):
            if c < CHUNKS - 1:
                bank = ps.tile([P, BANK], F32, name="b_bank%d" % c)
            else:
                bank = ps.tile([P, T], F32, name="b_last", tag="late")
            score(bank[:, 0:N], codes2, scales2, c)
            if c in (0, CHUNKS - 1):
                nc.scalar.activation(b_sb[:, c * N : (c + 1) * N], bank[:, 0:N], ACT.Copy)
            else:
                nc.vector.tensor_copy(b_sb[:, c * N : (c + 1) * N], bank[:, 0:N])
        codes1, scales1 = quantise(grouped1, "1")

        x = sb.tile([P, I], F32, name="x")
        e = sb.tile([P, I], F32, name="e")
        nc.scalar.activation(e[:], b_sb[:].indirect(list2[:]), ACT.Exp)
        nc.vector.tensor_copy(x[:], b_sb[:].indirect(list2[:]))

        a_sb = sb.tile([P, T], F32, name="a_sb")
        a_banks = ps.tile([P, T], F32, name="a_banks", tag="late")
        for c in range(CHUNKS):
            score(a_banks[:, c * N : (c + 1) * N], codes1, scales1, c)
        nc.vector.tensor_copy(a_sb[:, 0:BANK], a_banks[:, 0:BANK])
        e1 = sb.tile([P, I], F32, name="e1")
        nc.vector.tensor_scalar(e1[:], e[:], EXP_CAP, 1.0, ALU.min, ALU.add)
        nc.vector.tensor_copy(a_sb[:, BANK:T], a_banks[:, BANK:T])
        ag = sb.tile([P, I], F32, name="ag")
        nc.vector.tensor_copy(ag[:], a_sb[:].indirect(list1[:]))

        capped = sb.tile([P, I], F32, name="capped")
        den = sb.tile([P, I], F32, name="den")
        num = sb.tile([P, I], F32, name="num")
        for lo in (0, HALF):
            s = slice(lo, lo + HALF)
            nc.scalar.activation(capped[:, s], e1[:, s], ACT.Ln, scale=math.exp(0.5))
            nc.vector.scalar_tensor_tensor(den[:, s], x[:, s], 0.5, capped[:, s], ALU.add, ALU.max)
        nc.vector.tensor_scalar(num[:], ag[:], lam_col[:], None, ALU.mult)

        root = sb.tile([P, I], F32, name="root")
        inv = sb.tile([P, I], F32, name="inv")
        for lo, hi in ((0, QUARTER), (QUARTER, I - QUARTER), (I - QUARTER, I)):
            s = slice(lo, hi)
            nc.scalar.activation(root[:, s], den[:, s], ACT.Abs_reciprocal_sqrt)
            nc.scalar.activation(inv[:, s], root[:, s], ACT.Square)
        for lo, hi in ((0, QUARTER), (QUARTER, I)):
            s = slice(lo, hi)
            nc.vector.tensor_tensor(listed(f1, list1, lo, hi), num[:, s], inv[:, s], ALU.mult)

        f2 = sb.tile([P, T], F32, name="f2")
        nc.vector.tensor_tensor(f2[:], f1[:], old_sb[:], ALU.add)

        g3 = sb.tile([P, I], F32, name="g3")
        g4 = sb.tile([P, I], F32, name="g4")
        y = sb.tile([P, I], F32, name="y")
        for lo in (0, HALF):
            s = slice(lo, lo + HALF)
            nc.scalar.activation(g4[:, s], listed(f2, list4, lo, lo + HALF), ACT.Copy)
            nc.vector.tensor_copy(g3[:, s], listed(f2, list3, lo, lo + HALF))
            nc.vector.tensor_tensor(y[:, s], g3[:, s], g4[:, s], ALU.max)
            nc.sync.dma_start(out=out[:, s], in_=y[:, s])
